import numpy as np
import ml_dtypes


def mxq(x, axis, fmt="e4m3"):
    dtype, down = {"e4m3": (ml_dtypes.float8_e4m3fn, 7), "e5m2": (ml_dtypes.float8_e5m2, 14)}[fmt]
    v = np.moveaxis(np.asarray(x, np.float32).astype(ml_dtypes.bfloat16).astype(np.float64), axis, -1)
    blocks = v.reshape(v.shape[:-1] + (-1, 32))
    amax = np.abs(blocks).max(-1, keepdims=True)
    byte = np.maximum(np.where(amax > 0, np.frexp(amax)[1] - 1 + 127, 0) - down, 1)
    scale = np.exp2(byte - 127.0)
    codes = (blocks / scale).astype(np.float32).astype(dtype).astype(np.float64)
    return np.moveaxis((codes * scale).reshape(v.shape), -1, axis)


WIDE = False


def mx_kscale(k):
    if not WIDE:
        return np.ones(k)
    levels = np.array([10, -10, 5, -5, 0])
    if k % 512:
        return np.exp2(np.random.permutation(np.resize(levels, k // 32))).repeat(32)
    a = np.empty((k // 512, 16))
    for p in range(k // 512):
        a[p, :8] = np.random.permutation(np.resize(levels, 8))
        for g in range(8):
            far = levels[np.abs(levels - a[p, g]) >= 10]
            a[p, g + 8] = far[np.random.randint(len(far))]
    return np.exp2(a.ravel()).repeat(32)


BF16 = ml_dtypes.bfloat16


def bf(x):
    return np.asarray(x, np.float32).astype(BF16)


def f64(x):
    return np.asarray(x).astype(np.float64)


E2M1 = np.array([0.0, 0.5, 1.0, 1.5, 2.0, 3.0, 4.0, 6.0, -0.0, -0.5, -1.0, -1.5, -2.0, -3.0, -4.0, -6.0])


def pack_weight(w, fmt):
    k, n = w.shape
    w = f64(bf(w)).reshape(k // 32, 32, n)
    amax = np.abs(w).max(1)
    if fmt == "e4m3":
        byte = np.frexp(amax)[1] - 1 + 127 - 7
    else:
        mant, ex = np.frexp(amax / 6.0)
        byte = np.where(mant > 0.5, ex, ex - 1) + 127
    byte = np.clip(np.where(amax > 0, byte, 1), 1, 254)
    scaled = (w * np.exp2(127.0 - byte)[:, None, :]).reshape(k, n).astype(np.float32)
    by_word = np.ascontiguousarray(scaled.reshape(k // 512, 128, 4, n).transpose(0, 1, 3, 2))
    if fmt == "e4m3":
        words = by_word.astype(ml_dtypes.float8_e4m3fn).view(np.uint8)
    else:
        c = by_word.astype(ml_dtypes.float4_e2m1fn).view(np.uint8) & 0xF
        words = c[..., 0::2] | (c[..., 1::2] << 4)
    return np.ascontiguousarray(words), np.ascontiguousarray(byte.astype(np.uint8).reshape(k // 512, 16, n))


def unpack_weight(words, scales, fmt):
    g, p, n, _ = words.shape
    if fmt == "e4m3":
        vals = np.ascontiguousarray(words).view(ml_dtypes.float8_e4m3fn).astype(np.float64)
    else:
        nib = np.empty((g, p, n, 4), np.uint8)
        nib[..., 0::2] = words & 0xF
        nib[..., 1::2] = words >> 4
        vals = E2M1[nib]
    vals = vals * np.repeat(np.exp2(scales.astype(np.float64) - 127.0), 8, axis=1)[..., None]
    return vals.transpose(0, 1, 3, 2).reshape(g * 512, n)
def pack4(w):
    words, scales = pack_weight(w, "e2m1")
    return words.reshape(words.shape[0], 128, -1), scales


def unpack4(words, scales):
    return unpack_weight(words.reshape(words.shape[0], 128, -1, 2), scales, "e2m1")


B, U, Y, R = 1024, 1024, 1536, 512


def draw0():
    s = mx_kscale(U)
    t = mx_kscale(Y)
    c = mx_kscale(B)
    u = np.random.standard_normal((B, U)) * s * c[:, None]
    plant = np.random.standard_normal((U, Y)) / np.sqrt(U) / s[:, None] * t
    ref = np.random.standard_normal((B, Y)) * t * c[:, None]
    keep = (1 + 0.1 * np.random.standard_normal(U)) / s
    learn = np.random.standard_normal((Y, U)) / np.sqrt(Y) / t[:, None]
    modes = np.random.standard_normal((R, B)) / np.sqrt(B) / c
    l_words, l_scales = pack4(learn)
    return {"u": bf(u), "plant": bf(plant), "ref": bf(ref), "keep": bf(keep),
            "l_words": l_words, "l_scales": l_scales, "modes": bf(modes)}


def core(u, plant, ref, keep, l_words, l_scales, modes):
    y = mxq(f64(u), 1, "e4m3") @ mxq(f64(plant), 0, "e4m3")
    e = f64(ref) - y
    step = mxq(e, 1, "e4m3") @ unpack4(l_words, l_scales)
    u_next = f64(u) * f64(keep) + step
    z = mxq(f64(modes), 1, "e4m3") @ mxq(e, 0, "e4m3")
    return u_next, z


def e4m3fn_bytes(y):
    return np.clip(np.asarray(y, np.float64), -448.0, 448.0).astype(np.float32).astype(ml_dtypes.float8_e4m3fn).view(np.uint8)


def e4m3fn_values(b):
    return np.asarray(b, np.uint8).view(ml_dtypes.float8_e4m3fn).astype(np.float64)


def setup_inputs():
    d = draw0()
    x0 = np.asarray(d['modes']).astype(np.float64)
    s = (np.max(np.abs(x0), axis=(0,), keepdims=True) / 448.0).astype(np.float32)
    out = {}
    for k, v in d.items():
        if k == 'modes':
            out['modes_bytes'] = e4m3fn_bytes(x0 / s.astype(np.float64))
            out['modes_scale'] = s
        else:
            out[k] = v
    return out


def reference(u, plant, ref, keep, l_words, l_scales, modes_bytes, modes_scale):
    return core(u, plant, ref, keep, l_words, l_scales, e4m3fn_values(modes_bytes) * modes_scale.astype(np.float64))

@@ -1,0 +1,271 @@
+from contextlib import ExitStack
+
+import concourse.mybir as mybir
+from concourse.masks import make_identity
+
+F32 = mybir.dt.float32
+BF16 = mybir.dt.bfloat16
+I32 = mybir.dt.int32
+U32 = mybir.dt.uint32
+U8 = mybir.dt.uint8
+F8 = mybir.dt.float8_e4m3fn
+FP8X4 = mybir.dt.float8_e4m3fn_x4
+FP4X4 = mybir.dt.float4_e2m1fn_x4
+MULT = mybir.AluOpType.mult
+ADD = mybir.AluOpType.add
+SUB = mybir.AluOpType.subtract
+
+B, U, Y, R = 1024, 1024, 1536, 512
+P = 128
+KP = 512
+NT = 512
+G, KG, C = B // KP, U // KP, Y // NT
+PLANT_ENGINE = (("VV", "PP"), ("VS", "SP"), ("SS", "PP"))
+E_ENGINE = (("VV", "SS", "SS"), ("SS", "SS", "VV"))
+UK_ENGINE = "GG"
+LOADS = (('u', 0, 1), ('u', 0, 0), ('p', 0, 0), ('p', 0, 1), ('r', 0, 0), ('p', 1, 0), ('p', 1, 1), ('r', 0, 1), ('p', 2, 0), ('p', 2, 1), ('u', 1, 0), ('u', 1, 1), ('r', 0, 2), ('r', 1, 0), ('l',), ('s',), ('m',), ('r', 1, 1), ('r', 1, 2))
+IL_BUFS = 8
+SCHED = (('UT', 0, 0), ('UT', 0, 1), ('PI', 0, 0), ('PI', 0, 1), ('GN', 0, 0), ('GN', 0, 1), ('GN', 0, 2), ('GN', 0, 3), ('ER', 0, 0, 0), ('ER', 0, 0, 1), ('ER', 0, 0, 2), ('ER', 0, 0, 3), ('PI', 1, 0), ('PI', 1, 1), ('ER', 0, 1, 0), ('ER', 0, 1, 1), ('ER', 0, 1, 2), ('ER', 0, 1, 3), ('ET', 0, 0), ('PI', 2, 0), ('PI', 2, 1), ('UT', 1, 0), ('UT', 1, 1), ('GN', 1, 0), ('GN', 1, 1), ('GN', 1, 2), ('GN', 1, 3), ('ET', 0, 1), ('ES', 0, 0), ('ER', 0, 2, 0), ('ER', 0, 2, 1), ('ER', 0, 2, 2), ('ER', 0, 2, 3), ('ER', 1, 0, 0), ('ER', 1, 0, 1), ('ER', 1, 0, 2), ('ER', 1, 0, 3), ('ES', 0, 1), ('ET', 0, 2), ('ES', 1, 0), ('ER', 1, 1, 0), ('ER', 1, 1, 1), ('ER', 1, 1, 2), ('ER', 1, 1, 3), ('ET', 1, 0), ('ES', 0, 2), ('MM', 0), ('MM', 1), ('MM', 2), ('MM', 3), ('ST', 0, 0, 0), ('ST', 0, 0, 1), ('ST', 0, 1, 0), ('ST', 0, 1, 1), ('MT', 0), ('MT', 1), ('ER', 1, 2, 0), ('ER', 1, 2, 1), ('ER', 1, 2, 2), ('ER', 1, 2, 3), ('ST', 0, 2, 0), ('ST', 0, 2, 1), ('ST', 0, 3, 0), ('ST', 0, 3, 1), ('ET', 1, 1), ('ES', 1, 1), ('PJ', 0, 0), ('PJ', 0, 1), ('PJ', 0, 2), ('PJ', 0, 3), ('ET', 1, 2), ('ES', 1, 2), ('PJ', 1, 0), ('PJ', 1, 1), ('PJ', 1, 2), ('PJ', 1, 3), ('ST', 1, 0, 0), ('ST', 1, 0, 1), ('ST', 1, 1, 0), ('ST', 1, 1, 1), ('PJ', 2, 0), ('PJ', 2, 1), ('PJ', 2, 2), ('PJ', 2, 3), ('ST', 1, 2, 0), ('ST', 1, 2, 1), ('ST', 1, 3, 0), ('ST', 1, 3, 1))
+FLOPS = 2 * (B * U * Y + B * Y * U + R * B * Y)
+
+
+def tile_fleet_learning_control_s8_kernel(
+    tc, u, plant, ref, keep, l_words, l_scales, modes_bytes, modes_scale, u_next, z
+):
+    nc = tc.nc
+    with ExitStack() as ctx:
+        one = ctx.enter_context(tc.tile_pool(name="one", bufs=1))
+        il_pool = ctx.enter_context(tc.tile_pool(name="il", bufs=1))
+        trp = ctx.enter_context(tc.psum_pool(name="trp", bufs=3))
+        mmp = ctx.enter_context(tc.psum_pool(name="mmp", bufs=5))
+
+        def keep_tile(shape, dtype, name):
+            return one.tile(shape, dtype, name=name, align_bytes=64)
+
+        krow = keep_tile([P, U], BF16, "krow")
+        nc.vector.memset(krow[:], 0.0)
+        nc.scalar.dma_start(out=krow[0:1, :], in_=keep.rearrange("(o k) -> o k", o=1))
+        ones = keep_tile([P, P], BF16, "ones")
+        nc.vector.memset(ones[:], 1.0)
+        ident = keep_tile([P, P], F32, "ident")
+        make_identity(nc, ident[:])
+        ident_b = keep_tile([P, P], BF16, "ident_b")
+        nc.vector.tensor_copy(out=ident_b[:], in_=ident[:])
+        lsc = keep_tile([P, C, U], U8, "lsc")
+        nc.gpsimd.memset(lsc[:].rearrange("p g n -> p (g n)").bitcast(I32), 0)
+
+        u_raw = [keep_tile([P, 4, U], BF16, f"u_raw{g}") for g in range(G)]
+        pl_raw = [
+            [il_pool.tile([P, 4, NT], BF16, name="pl", tag="pl", bufs=6, align_bytes=64) for k in range(KG)]
+            for c in range(C)
+        ]
+        rf = [[keep_tile([P, 4, NT], BF16, f"rf{g}_{c}") for c in range(C)] for g in range(G)]
+
+        def load_u(g, h):
+            src = u[g * KP : (g + 1) * KP, :].rearrange("(p t) k -> p t k", t=4)
+            if True:
+                nc.sync.dma_start(out=u_raw[g][:, 2 * h : 2 * h + 2, :], in_=src[:, 2 * h : 2 * h + 2, :])
+
+        def load_plant(c, k):
+            if True:
+                src = plant[k * KP : (k + 1) * KP, c * NT : (c + 1) * NT].rearrange("(p j) y -> p j y", j=4)
+                nc.sync.dma_start(out=pl_raw[c][k][:], in_=src)
+
+        def load_ref(g, c):
+            src = ref[g * KP : (g + 1) * KP, c * NT : (c + 1) * NT].rearrange("(p t) y -> p t y", t=4)
+            nc.sync.dma_start(out=rf[g][c][:], in_=src)
+
+        mb = keep_tile([P, 4, B], U8, "mb")
+        msc = keep_tile([P, B], F32, "msc")
+
+        def load_modes():
+            nc.sync.dma_start(out=msc[:], in_=modes_scale.rearrange("o k -> (o k)").partition_broadcast(P))
+            nc.sync.dma_start(out=mb[:], in_=modes_bytes.rearrange("(r p) k -> p r k", p=P))
+
+        lw = keep_tile([P, C, 2 * U], U8, "lw")
+
+        def load_l():
+            nc.sync.dma_start(out=lw[:], in_=l_words.rearrange("g p n -> p g n"))
+
+        def load_ls():
+            for q in range(4):
+                nc.sync.dma_start(
+                    out=lsc[32 * q : 32 * q + 4, :, :].bitcast(I32),
+                    in_=l_scales[:, 4 * q : 4 * q + 4, :].rearrange("g q n -> q g n").bitcast(I32),
+                )
+
+        for name, *args in LOADS:
+            {"u": load_u, "p": load_plant, "r": load_ref, "l": load_l, "s": load_ls, "m": load_modes}[name](*args)
+
+        keep_b = keep_tile([P, U], BF16, "keep_b")
+        for n in range(2):
+            acc = mmp.tile([P, NT], F32, name="acc")
+            nc.tensor.matmul(out=acc[:], lhsT=ones[:], rhs=krow[:, n * NT : (n + 1) * NT], start=True, stop=True)
+            nc.scalar.copy(out=keep_b[:, n * NT : (n + 1) * NT], in_=acc[:])
+
+        def codes(name):
+            return keep_tile([P, NT], U32, name + "_q"), keep_tile([P, NT], U8, name + "_s")
+
+        def quant(dst, il):
+            nc.vector.quantize_mx(out=dst[0][:].bitcast(FP8X4), scales=dst[1][:], in_=il[:])
+
+        def il_tile():
+            return il_pool.tile([P, 4 * NT], BF16, name="il", tag="il", bufs=IL_BUFS, align_bytes=64)
+
+        def turn(src, k0, sorted_words=False):
+            il = il_tile()
+            for h in range(2):
+                tr = trp.tile([P, NT], F32, name="tr")
+                for s in range(2):
+                    words = src[:, 2 * h + s, k0 : k0 + KP].bitcast(F32)
+                    for w in range(2):
+                        b0 = (2 * s + w) * P
+                        cols = words[:, w * P : (w + 1) * P] if sorted_words else words[:, w : KP // 2 : 2]
+                        nc.tensor.transpose(tr[:, b0 : b0 + P], cols, ident[:])
+                nc.scalar.copy(
+                    out=il[:, h * 1024 : (h + 1) * 1024].bitcast(F32).rearrange("p (s b u) -> p s b u", s=2, u=2),
+                    in_=tr[:].rearrange("p (s u b) -> p s b u", s=2, u=2),
+                )
+            return il
+
+        def spread_half(il, src, h, engine):
+            cols = slice(h * 256, h * 256 + 256)
+            out = il[:, h * 1024 : h * 1024 + 1024].rearrange("p (c i j) -> p c j i", i=4, j=4)
+            in_ = src[:, :, cols].rearrange("p j (c i) -> p c j i", i=4)
+            if engine == "V":
+                nc.vector.tensor_copy(out=out, in_=in_)
+            elif engine == "S":
+                nc.scalar.copy(out=out, in_=in_)
+            else:
+                in_ = src[:, :, cols].rearrange("p j c -> p c j")
+                mid = trp.tile([P, 1024], BF16, name="tr")
+                for q in range(2):
+                    nc.tensor.matmul(
+                        out=mid[:, q * NT : (q + 1) * NT],
+                        lhsT=ident_b[:],
+                        rhs=in_[:, q * P : (q + 1) * P, :],
+                        start=True,
+                        stop=True,
+                    )
+                nc.scalar.copy(out=il[:, h * 1024 : (h + 1) * 1024], in_=mid[:])
+
+        def spread(src, engines):
+            il = il_tile()
+            if engines[0] == engines[1] and engines[0] != "P":
+                out = il[:].rearrange("p (c i j) -> p c j i", i=4, j=4)
+                in_ = src[:].rearrange("p j (c i) -> p c j i", i=4)
+                if engines[0] == "V":
+                    nc.vector.tensor_copy(out=out, in_=in_)
+                else:
+                    nc.scalar.copy(out=out, in_=in_)
+            else:
+                for h in range(2):
+                    spread_half(il, src, h, engines[h])
+            return il
+
+        def mx(out, lhs, m0, rhs, n, start, stop):
+            nc.tensor.matmul_mx(
+                out=out,
+                lhsT=lhs[0][:, m0 : m0 + P].bitcast(FP8X4),
+                lhsT_scale=lhs[1][:, m0 : m0 + P],
+                rhs=rhs[0][:, 0:n].bitcast(FP8X4),
+                rhs_scale=rhs[1][:, 0:n],
+                start=start,
+                stop=stop,
+            )
+
+        uq = [[codes(f"u{g}{k}") for k in range(KG)] for g in range(G)]
+        pq = [[codes(f"p{c}{k}") for k in range(KG)] for c in range(C)]
+        etq = [[codes(f"et{g}{c}") for c in range(C)] for g in range(G)]
+        ebq = [[codes(f"eb{g}{c}") for c in range(C)] for g in range(G)]
+        mq = [codes(f"m{g}") for g in range(G)]
+        e_pl = {}
+
+        def u_in(g, k):
+            il = turn(u_raw[g], k * KP)
+            quant(uq[g][k], il)
+
+        def plant_in(c, k):
+            il = spread(pl_raw[c][k], PLANT_ENGINE[c][k])
+            quant(pq[c][k], il)
+
+        def err(g, c, t):
+            if (g, c) not in e_pl:
+                e_pl[g, c] = il_pool.tile([P, 4, NT], BF16, name="e_pl", tag="e_pl", bufs=6, align_bytes=64)
+            e = e_pl[g, c]
+            if True:
+                acc = mmp.tile([P, NT], F32, name="acc")
+                for k in range(KG):
+                    mx(acc[:], uq[g][k], t * P, pq[c][k], NT, k == 0, k == KG - 1)
+                nc.vector.tensor_tensor(
+                    out=e[:, t, :].rearrange("p (w b x) -> p w b x", w=2, x=2),
+                    in0=rf[g][c][:, t, :].rearrange("p (b w x) -> p w b x", w=2, x=2),
+                    in1=acc[:].rearrange("p (b w x) -> p w b x", w=2, x=2),
+                    op=SUB,
+                )
+
+        def err_turn(g, c):
+            il = turn(e_pl[g, c], 0, True)
+            quant(etq[g][c], il)
+
+        def err_spread(g, c):
+            il = spread(e_pl[g, c], E_ENGINE[g][c])
+            quant(ebq[g][c], il)
+
+        uks = {}
+
+        def gain(g, t):
+            if g == 0:
+                uk = il_pool.tile([P, U], F32, name="uk", tag="uk", bufs=4)
+            else:
+                uk = il_pool.tile([P, U], F32, name="pl", tag="pl", bufs=6, align_bytes=64)
+            uks[g, t] = uk
+            for n in range(4):
+                cols = slice(n * 256, (n + 1) * 256)
+                engine = nc.vector if UK_ENGINE[g] == "V" else nc.gpsimd
+                engine.tensor_tensor(out=uk[:, cols], in0=u_raw[g][:, t, cols], in1=keep_b[:, cols], op=MULT)
+
+        def step(g, t, n):
+            uk = uks[g, t]
+            if True:
+                acc = mmp.tile([P, NT], F32, name="acc")
+                cols = slice(n * NT, (n + 1) * NT)
+                for c in range(C):
+                    nc.tensor.matmul_mx(
+                        out=acc[:],
+                        lhsT=etq[g][c][0][:, t * P : (t + 1) * P].bitcast(FP8X4),
+                        lhsT_scale=etq[g][c][1][:, t * P : (t + 1) * P],
+                        rhs=lw[:, c, 2 * n * NT : 2 * (n + 1) * NT].bitcast(FP4X4),
+                        rhs_scale=lsc[:, c, cols],
+                        start=c == 0,
+                        stop=c == C - 1,
+                    )
+                nc.vector.tensor_tensor(out=uk[:, cols], in0=acc[:], in1=uk[:, cols], op=ADD)
+            dst = u_next[g * KP : (g + 1) * KP, :].rearrange("(p t) k -> p t k", t=4)
+            nc.sync.dma_start(out=dst[:, t, cols], in_=uk[:, cols])
+
+        mbf = keep_tile([P, 4, B], BF16, "mbf")
+
+        def modes_mul(r):
+            nc.vector.tensor_tensor(out=mbf[:, r, :], in0=mb[:, r, :].bitcast(F8), in1=msc[:], op=MULT)
+
+        def modes_in(g):
+            il = turn(mbf, g * KP)
+            quant(mq[g], il)
+
+        def proj(c, r):
+            acc = mmp.tile([P, NT], F32, name="acc")
+            for g in range(G):
+                mx(acc[:], mq[g], r * P, ebq[g][c], NT, g == 0, g == G - 1)
+            zt = il_pool.tile([P, NT], F32, name="zt", tag="zt", bufs=4)
+            nc.scalar.copy(
+                out=zt[:].rearrange("p (b w x) -> p b w x", w=2, x=2),
+                in_=acc[:].rearrange("p (w b x) -> p b w x", w=2, x=2),
+            )
+            nc.sync.dma_start(out=z[r * P : (r + 1) * P, c * NT : (c + 1) * NT], in_=zt[:])
+
+        for name, *args in SCHED:
+            {
+                "UT": u_in, "PI": plant_in, "ER": err, "ET": err_turn, "ES": err_spread,
+                "MM": modes_mul, "MT": modes_in, "GN": gain, "ST": step, "PJ": proj,
+            }[name](*args)

@@ -20,12 +20,12 @@ P = 128
 KP = 512
 NT = 512
 G, KG, C = B // KP, U // KP, Y // NT
-PLANT_ENGINE = (("VV", "PP"), ("VS", "SP"), ("SS", "PP"))
-E_ENGINE = (("VV", "SS", "SS"), ("SS", "SS", "VV"))
-UK_ENGINE = "GG"
-LOADS = (('u', 0, 1), ('u', 0, 0), ('p', 0, 0), ('p', 0, 1), ('r', 0, 0), ('p', 1, 0), ('p', 1, 1), ('r', 0, 1), ('p', 2, 0), ('p', 2, 1), ('u', 1, 0), ('u', 1, 1), ('r', 0, 2), ('r', 1, 0), ('l',), ('s',), ('m',), ('r', 1, 1), ('r', 1, 2))
+PLANT_ENGINE = (("VV","SP"),("PP","SP"),("SS","SP"))
+E_ENGINE = (("SP","SS","SS"),("SS","SV","SS"))
+UK_ENGINE = "VV"
+LOADS = (("u",0,0),("u",0,1),("k",),("p",0,0,1),("p",1,0,1),("p",0,1,3),("p",1,1,3),("r",0,0,1),("r",0,1,3),("u",1,0),("u",1,1),("m",),("s",),("l",),("r",1,0,3))
 IL_BUFS = 8
-SCHED = (('UT', 0, 0), ('UT', 0, 1), ('PI', 0, 0), ('PI', 0, 1), ('GN', 0, 0), ('GN', 0, 1), ('GN', 0, 2), ('GN', 0, 3), ('ER', 0, 0, 0), ('ER', 0, 0, 1), ('ER', 0, 0, 2), ('ER', 0, 0, 3), ('PI', 1, 0), ('PI', 1, 1), ('ER', 0, 1, 0), ('ER', 0, 1, 1), ('ER', 0, 1, 2), ('ER', 0, 1, 3), ('ET', 0, 0), ('PI', 2, 0), ('PI', 2, 1), ('UT', 1, 0), ('UT', 1, 1), ('GN', 1, 0), ('GN', 1, 1), ('GN', 1, 2), ('GN', 1, 3), ('ET', 0, 1), ('ES', 0, 0), ('ER', 0, 2, 0), ('ER', 0, 2, 1), ('ER', 0, 2, 2), ('ER', 0, 2, 3), ('ER', 1, 0, 0), ('ER', 1, 0, 1), ('ER', 1, 0, 2), ('ER', 1, 0, 3), ('ES', 0, 1), ('ET', 0, 2), ('ES', 1, 0), ('ER', 1, 1, 0), ('ER', 1, 1, 1), ('ER', 1, 1, 2), ('ER', 1, 1, 3), ('ET', 1, 0), ('ES', 0, 2), ('MM', 0), ('MM', 1), ('MM', 2), ('MM', 3), ('ST', 0, 0, 0), ('ST', 0, 0, 1), ('ST', 0, 1, 0), ('ST', 0, 1, 1), ('MT', 0), ('MT', 1), ('ER', 1, 2, 0), ('ER', 1, 2, 1), ('ER', 1, 2, 2), ('ER', 1, 2, 3), ('ST', 0, 2, 0), ('ST', 0, 2, 1), ('ST', 0, 3, 0), ('ST', 0, 3, 1), ('ET', 1, 1), ('ES', 1, 1), ('PJ', 0, 0), ('PJ', 0, 1), ('PJ', 0, 2), ('PJ', 0, 3), ('ET', 1, 2), ('ES', 1, 2), ('PJ', 1, 0), ('PJ', 1, 1), ('PJ', 1, 2), ('PJ', 1, 3), ('ST', 1, 0, 0), ('ST', 1, 0, 1), ('ST', 1, 1, 0), ('ST', 1, 1, 1), ('PJ', 2, 0), ('PJ', 2, 1), ('PJ', 2, 2), ('PJ', 2, 3), ('ST', 1, 2, 0), ('ST', 1, 2, 1), ('ST', 1, 3, 0), ('ST', 1, 3, 1))
+SCHED = (("UTp",0,1,0),("UTp",0,1,1),("UTs",0,1,0),("UTs",0,1,1),("UTq",0,1,0),("PIp",0,0,0),("PIp",0,0,1),("PIs",0,0,0),("KBp",1),("KBs",1),("PIs",0,0,1),("UTq",0,1,1),("KBp",0),("KBs",0),("PIq",0,0),("GN",0,2),("UTp",0,0,0),("UTp",0,0,1),("UTs",0,0,0),("UTs",0,0,1),("PIp",0,1,0),("PIp",0,1,1),("PIs",0,1,0),("UTq",0,0,0),("MSp",1),("GN",0,0),("PIs",0,1,1),("PIp",1,0,0),("PIp",1,0,1),("PIs",1,0,0),("MSs",1),("UTq",0,0,1),("GN",0,1),("PIs",1,0,1),("PIq",0,1),("GN",0,3),("MSp",0),("ERp",0,0,0),("PIq",1,0),("PIp",1,1,0),("PIp",1,1,1),("PIs",1,1,0),("MSs",0),("ERv",0,0,0),("ERp",0,0,3),("PIs",1,1,1),("ERp",0,0,1),("ERv",0,0,3),("PIp",2,1,0),("PIp",2,1,1),("PIs",2,1,0),("PIq",1,1),("ERv",0,0,1),("ERp",0,0,2),("PIs",2,1,1),("ERp",0,1,2),("ERv",0,0,2),("ERp",0,1,3),("PIq",2,1),("ERv",0,1,2),("ERp",0,1,0),("ERv",0,1,3),("ERp",0,1,1),("ERv",0,1,0),("PIp",2,0,0),("PIp",2,0,1),("PIs",2,0,0),("ERv",0,1,1),("PIs",2,0,1),("ESp",0,0,0),("ESp",0,0,1),("UTp",1,1,0),("UTp",1,1,1),("ESs",0,0,1),("UTs",1,1,0),("UTs",1,1,1),("PIq",2,0),("UTp",1,0,0),("UTp",1,0,1),("UTs",1,0,0),("UTs",1,0,1),("ERp",0,2,2),("MMv",1),("ESs",0,0,0),("UTq",1,1,1),("ERv",0,2,2),("ETp",0,1,0),("ETp",0,1,1),("ETs",0,1,0),("ETs",0,1,1),("UTq",1,0,1),("ERp",0,2,0),("MMv",2),("ESq",0,0),("ERp",0,2,1),("ERv",0,2,0),("ERp",0,2,3),("ERv",0,2,1),("ETp",0,0,0),("ETp",0,0,1),("ETs",0,0,0),("ETs",0,0,1),("ERv",0,2,3),("ERp",1,0,1),("ETq",0,1),("ERp",1,0,2),("ERv",1,0,1),("ETp",0,2,0),("ETp",0,2,1),("ETs",0,2,0),("ETs",0,2,1),("ERv",1,0,2),("ERp",1,0,3),("ERp",1,0,0),("ETq",0,0),("ERv",1,0,3),("ERp",1,2,3),("ERv",1,0,0),("ERp",1,1,1),("ERv",1,2,3),("ERp",1,1,3),("ETq",0,2),("ERv",1,1,1),("ERp",1,2,0),("ERv",1,1,3),("ERp",1,2,2),("ERv",1,2,0),("ERv",1,2,2),("ESp",0,1,0),("ESp",0,1,1),("ESs",0,1,1),("ESp",0,2,0),("ESp",0,2,1),("STp",0,1,0),("STv",0,1,0),("ESs",0,2,1),("ERp",1,1,2),("ESs",0,1,0),("ERv",1,1,2),("ESs",0,2,0),("ERp",1,2,1),("MMv",0),("STp",0,2,0),("STv",0,2,0),("MMv",3),("ESq",0,1),("ERv",1,2,1),("ESq",0,2),("ESp",1,0,0),("ESp",1,0,1),("STp",0,0,1),("STv",0,0,1),("ESs",1,0,1),("ERp",1,1,0),("ERv",1,1,0),("ESp",1,1,0),("ESp",1,1,1),("STp",0,0,0),("STv",0,0,0),("ESs",1,0,0),("ESs",1,1,1),("ETp",1,0,0),("ETp",1,0,1),("ETs",1,0,0),("ETs",1,0,1),("MTp",1,0),("MTp",1,1),("MTs",1,0),("MTs",1,1),("MTq",1),("MTp",0,0),("MTp",0,1),("MTs",0,0),("MTs",0,1),("MTq",0),("ESq",1,0),("ESs",1,1,0),("STp",0,2,1),("STv",0,2,1),("ETp",1,1,0),("ETp",1,1,1),("ETs",1,1,0),("ETs",1,1,1),("STp",0,3,0),("STv",0,3,0),("ESq",1,1),("ETq",1,0),("ETp",1,2,0),("ETp",1,2,1),("ETs",1,2,0),("ETs",1,2,1),("PJp",0,0),("PJs",0,0),("PJp",0,1),("PJs",0,1),("PJp",0,2),("PJs",0,2),("ETq",1,1),("STp",0,1,1),("STv",0,1,1),("PJp",1,0),("PJs",1,0),("ETq",1,2),("GN",1,2),("PJp",1,3),("PJs",1,3),("GN",1,1),("PJp",1,2),("PJs",1,2),("ESp",1,2,0),("ESp",1,2,1),("PJp",1,1),("PJs",1,1),("ESs",1,2,1),("STp",1,2,1),("STv",1,2,1),("STp",0,3,1),("STv",0,3,1),("GN",1,0),("ESs",1,2,0),("STp",1,1,0),("STv",1,1,0),("STp",1,0,1),("STv",1,0,1),("PJp",0,3),("PJs",0,3),("ESq",1,2),("STp",1,2,0),("STv",1,2,0),("STp",1,1,1),("STv",1,1,1),("PJp",2,0),("PJs",2,0),("GN",1,3),("PJp",2,1),("PJs",2,1),("PJp",2,3),("PJs",2,3),("STp",1,3,1),("STv",1,3,1),("STp",1,3,0),("STv",1,3,0),("PJp",2,2),("PJs",2,2),("STp",1,0,0),("STv",1,0,0))
 FLOPS = 2 * (B * U * Y + B * Y * U + R * B * Y)
 
 
@@ -42,11 +42,6 @@ def tile_fleet_learning_control_s8_kernel(
         def keep_tile(shape, dtype, name):
             return one.tile(shape, dtype, name=name, align_bytes=64)
 
-        krow = keep_tile([P, U], BF16, "krow")
-        nc.vector.memset(krow[:], 0.0)
-        nc.scalar.dma_start(out=krow[0:1, :], in_=keep.rearrange("(o k) -> o k", o=1))
-        ones = keep_tile([P, P], BF16, "ones")
-        nc.vector.memset(ones[:], 1.0)
         ident = keep_tile([P, P], F32, "ident")
         make_identity(nc, ident[:])
         ident_b = keep_tile([P, P], BF16, "ident_b")
@@ -54,35 +49,41 @@ def tile_fleet_learning_control_s8_kernel(
         lsc = keep_tile([P, C, U], U8, "lsc")
         nc.gpsimd.memset(lsc[:].rearrange("p g n -> p (g n)").bitcast(I32), 0)
 
+        ctx.enter_context(tc.manual_schedule())
+        krow = il_pool.tile([P, U], BF16, name="krow", tag="zt", bufs=4)
+        nc.vector.memset(krow[:].bitcast(I32), 0)
+        mrow = keep_tile([P, B], F32, "mrow")
+        nc.vector.memset(mrow[:], 0.0)
+        ones = keep_tile([P, P], F32, "ones")
+        nc.vector.memset(ones[:], 1.0)
+        ones_b = keep_tile([P, P], BF16, "ones_b")
+        nc.vector.memset(ones_b[:], 1.0)
         u_raw = [keep_tile([P, 4, U], BF16, f"u_raw{g}") for g in range(G)]
-        pl_raw = [
-            [il_pool.tile([P, 4, NT], BF16, name="pl", tag="pl", bufs=6, align_bytes=64) for k in range(KG)]
-            for c in range(C)
-        ]
-        rf = [[keep_tile([P, 4, NT], BF16, f"rf{g}_{c}") for c in range(C)] for g in range(G)]
+        pl_raw = [keep_tile([P, 4, Y], BF16, f"pl{k}") for k in range(KG)]
+        rf = [keep_tile([P, 4, Y], BF16, f"rf{g}") for g in range(G)]
+        mb = keep_tile([P, 4, B], U8, "mb")
+        msc = keep_tile([P, B], F32, "msc")
+        lw = keep_tile([P, C, 2 * U], U8, "lw")
+        keep_b = keep_tile([P, U], BF16, "keep_b")
 
         def load_u(g, h):
             src = u[g * KP : (g + 1) * KP, :].rearrange("(p t) k -> p t k", t=4)
-            if True:
-                nc.sync.dma_start(out=u_raw[g][:, 2 * h : 2 * h + 2, :], in_=src[:, 2 * h : 2 * h + 2, :])
+            nc.sync.dma_start(out=u_raw[g][:, 2 * h : 2 * h + 2, :], in_=src[:, 2 * h : 2 * h + 2, :])
 
-        def load_plant(c, k):
-            if True:
-                src = plant[k * KP : (k + 1) * KP, c * NT : (c + 1) * NT].rearrange("(p j) y -> p j y", j=4)
-                nc.sync.dma_start(out=pl_raw[c][k][:], in_=src)
+        def load_plant(k, c0, c1):
+            src = plant[k * KP : (k + 1) * KP, c0 * NT : c1 * NT].rearrange("(p j) y -> p j y", j=4)
+            nc.sync.dma_start(out=pl_raw[k][:, :, c0 * NT : c1 * NT], in_=src)
 
-        def load_ref(g, c):
-            src = ref[g * KP : (g + 1) * KP, c * NT : (c + 1) * NT].rearrange("(p t) y -> p t y", t=4)
-            nc.sync.dma_start(out=rf[g][c][:], in_=src)
-
-        mb = keep_tile([P, 4, B], U8, "mb")
-        msc = keep_tile([P, B], F32, "msc")
+        def load_ref(g, c0, c1):
+            src = ref[g * KP : (g + 1) * KP, c0 * NT : c1 * NT].rearrange("(p t) y -> p t y", t=4)
+            nc.sync.dma_start(out=rf[g][:, :, c0 * NT : c1 * NT], in_=src)
 
         def load_modes():
-            nc.sync.dma_start(out=msc[:], in_=modes_scale.rearrange("o k -> (o k)").partition_broadcast(P))
-            nc.sync.dma_start(out=mb[:], in_=modes_bytes.rearrange("(r p) k -> p r k", p=P))
+            nc.sync.dma_start(out=mb[:], in_=modes_bytes.rearrange("(p r) k -> p r k", r=4))
 
-        lw = keep_tile([P, C, 2 * U], U8, "lw")
+        def load_rows():
+            nc.sync.dma_start(out=krow[0:1, :], in_=keep.rearrange("(o k) -> o k", o=1))
+            nc.sync.dma_start(out=mrow[0:1, :], in_=modes_scale)
 
         def load_l():
             nc.sync.dma_start(out=lw[:], in_=l_words.rearrange("g p n -> p g n"))
@@ -95,73 +96,71 @@ def tile_fleet_learning_control_s8_kernel(
                 )
 
         for name, *args in LOADS:
-            {"u": load_u, "p": load_plant, "r": load_ref, "l": load_l, "s": load_ls, "m": load_modes}[name](*args)
-
-        keep_b = keep_tile([P, U], BF16, "keep_b")
-        for n in range(2):
-            acc = mmp.tile([P, NT], F32, name="acc")
-            nc.tensor.matmul(out=acc[:], lhsT=ones[:], rhs=krow[:, n * NT : (n + 1) * NT], start=True, stop=True)
-            nc.scalar.copy(out=keep_b[:, n * NT : (n + 1) * NT], in_=acc[:])
+            {"u": load_u, "p": load_plant, "r": load_ref, "l": load_l, "s": load_ls, "m": load_modes, "k": load_rows}[name](*args)
 
         def codes(name):
             return keep_tile([P, NT], U32, name + "_q"), keep_tile([P, NT], U8, name + "_s")
 
-        def quant(dst, il):
-            nc.vector.quantize_mx(out=dst[0][:].bitcast(FP8X4), scales=dst[1][:], in_=il[:])
+        def quant(dst, il, h=None):
+            w = slice(0, NT) if h is None else slice(h * 256, h * 256 + 256)
+            e = slice(4 * w.start, 4 * w.stop)
+            nc.vector.quantize_mx(out=dst[0][:, w].bitcast(FP8X4), scales=dst[1][:, w], in_=il[:, e])
 
         def il_tile():
             return il_pool.tile([P, 4 * NT], BF16, name="il", tag="il", bufs=IL_BUFS, align_bytes=64)
 
-        def turn(src, k0, sorted_words=False):
-            il = il_tile()
-            for h in range(2):
-                tr = trp.tile([P, NT], F32, name="tr")
-                for s in range(2):
-                    words = src[:, 2 * h + s, k0 : k0 + KP].bitcast(F32)
-                    for w in range(2):
-                        b0 = (2 * s + w) * P
-                        cols = words[:, w * P : (w + 1) * P] if sorted_words else words[:, w : KP // 2 : 2]
-                        nc.tensor.transpose(tr[:, b0 : b0 + P], cols, ident[:])
-                nc.scalar.copy(
-                    out=il[:, h * 1024 : (h + 1) * 1024].bitcast(F32).rearrange("p (s b u) -> p s b u", s=2, u=2),
-                    in_=tr[:].rearrange("p (s u b) -> p s b u", s=2, u=2),
-                )
-            return il
+        ils = {}
+        banks = {}
 
-        def spread_half(il, src, h, engine):
+        def turn_pe(key, src, k0, h, sorted_words=False):
+            if key not in ils:
+                ils[key] = il_tile()
+            tr = trp.tile([P, NT], F32, name="tr")
+            banks[key, h] = tr
+            for s in range(2):
+                words = src[:, 2 * h + s, k0 : k0 + KP].bitcast(F32)
+                for w in range(2):
+                    b0 = (2 * s + w) * P
+                    cols = words[:, w * P : (w + 1) * P] if sorted_words else words[:, w : KP // 2 : 2]
+                    nc.tensor.transpose(tr[:, b0 : b0 + P], cols, ident[:])
+
+        def turn_out(key, h, engine="S"):
+            il = ils[key]
+            copy = nc.scalar.copy if engine == "S" else nc.vector.tensor_copy
+            copy(
+                out=il[:, h * 1024 : (h + 1) * 1024].bitcast(F32).rearrange("p (s b u) -> p s b u", s=2, u=2),
+                in_=banks[key, h][:].rearrange("p (s u b) -> p s b u", s=2, u=2),
+            )
+
+        def spread_half(key, src, h, engine):
+            if key not in ils:
+                ils[key] = il_tile()
+            il = ils[key]
             cols = slice(h * 256, h * 256 + 256)
             out = il[:, h * 1024 : h * 1024 + 1024].rearrange("p (c i j) -> p c j i", i=4, j=4)
             in_ = src[:, :, cols].rearrange("p j (c i) -> p c j i", i=4)
             if engine == "V":
                 nc.vector.tensor_copy(out=out, in_=in_)
-            elif engine == "S":
+            else:
                 nc.scalar.copy(out=out, in_=in_)
-            else:
-                in_ = src[:, :, cols].rearrange("p j c -> p c j")
-                mid = trp.tile([P, 1024], BF16, name="tr")
-                for q in range(2):
-                    nc.tensor.matmul(
-                        out=mid[:, q * NT : (q + 1) * NT],
-                        lhsT=ident_b[:],
-                        rhs=in_[:, q * P : (q + 1) * P, :],
-                        start=True,
-                        stop=True,
-                    )
-                nc.scalar.copy(out=il[:, h * 1024 : (h + 1) * 1024], in_=mid[:])
 
-        def spread(src, engines):
-            il = il_tile()
-            if engines[0] == engines[1] and engines[0] != "P":
-                out = il[:].rearrange("p (c i j) -> p c j i", i=4, j=4)
-                in_ = src[:].rearrange("p j (c i) -> p c j i", i=4)
-                if engines[0] == "V":
-                    nc.vector.tensor_copy(out=out, in_=in_)
-                else:
-                    nc.scalar.copy(out=out, in_=in_)
-            else:
-                for h in range(2):
-                    spread_half(il, src, h, engines[h])
-            return il
+        def through_pe(key, src, h):
+            if key not in ils:
+                ils[key] = il_tile()
+            mid = trp.tile([P, 1024], BF16, name="tr")
+            banks[key, h] = mid
+            in_ = src[:, :, h * 256 : h * 256 + 256].rearrange("p j c -> p c j")
+            for q in range(2):
+                nc.tensor.matmul(
+                    out=mid[:, q * NT : (q + 1) * NT],
+                    lhsT=ident_b[:],
+                    rhs=in_[:, q * P : (q + 1) * P, :],
+                    start=True,
+                    stop=True,
+                )
+
+        def through_out(key, h):
+            nc.scalar.copy(out=ils[key][:, h * 1024 : (h + 1) * 1024], in_=banks[key, h][:])
 
         def mx(out, lhs, m0, rhs, n, start, stop):
             nc.tensor.matmul_mx(
@@ -179,93 +178,154 @@ def tile_fleet_learning_control_s8_kernel(
         etq = [[codes(f"et{g}{c}") for c in range(C)] for g in range(G)]
         ebq = [[codes(f"eb{g}{c}") for c in range(C)] for g in range(G)]
         mq = [codes(f"m{g}") for g in range(G)]
-        e_pl = {}
-
-        def u_in(g, k):
-            il = turn(u_raw[g], k * KP)
-            quant(uq[g][k], il)
-
-        def plant_in(c, k):
-            il = spread(pl_raw[c][k], PLANT_ENGINE[c][k])
-            quant(pq[c][k], il)
-
-        def err(g, c, t):
-            if (g, c) not in e_pl:
-                e_pl[g, c] = il_pool.tile([P, 4, NT], BF16, name="e_pl", tag="e_pl", bufs=6, align_bytes=64)
-            e = e_pl[g, c]
-            if True:
-                acc = mmp.tile([P, NT], F32, name="acc")
-                for k in range(KG):
-                    mx(acc[:], uq[g][k], t * P, pq[c][k], NT, k == 0, k == KG - 1)
-                nc.vector.tensor_tensor(
-                    out=e[:, t, :].rearrange("p (w b x) -> p w b x", w=2, x=2),
-                    in0=rf[g][c][:, t, :].rearrange("p (b w x) -> p w b x", w=2, x=2),
-                    in1=acc[:].rearrange("p (b w x) -> p w b x", w=2, x=2),
-                    op=SUB,
-                )
-
-        def err_turn(g, c):
-            il = turn(e_pl[g, c], 0, True)
-            quant(etq[g][c], il)
-
-        def err_spread(g, c):
-            il = spread(e_pl[g, c], E_ENGINE[g][c])
-            quant(ebq[g][c], il)
-
+        e_pl = [
+            [il_pool.tile([P, 4, NT], BF16, name="e_pl", tag="e_pl", bufs=6, align_bytes=64) for c in range(C)]
+            for g in range(G)
+        ]
+        mbf = keep_tile([P, 4, B], BF16, "mbf")
         uks = {}
 
-        def gain(g, t):
+        def UTp(g, k, h):
+            turn_pe(("u", g, k), u_raw[g], k * KP, h)
+
+        def UTs(g, k, h):
+            turn_out(("u", g, k), h)
+
+        def UTq(g, k, h):
+            quant(uq[g][k], ils["u", g, k], h if g == 0 else None)
+
+        def PIp(c, k, h):
+            if PLANT_ENGINE[c][k][h] == "P":
+                through_pe(("p", c, k), pl_raw[k][:, :, c * NT : (c + 1) * NT], h)
+
+        def PIs(c, k, h):
+            if PLANT_ENGINE[c][k][h] == "P":
+                through_out(("p", c, k), h)
+            else:
+                spread_half(("p", c, k), pl_raw[k][:, :, c * NT : (c + 1) * NT], h, PLANT_ENGINE[c][k][h])
+
+        def PIq(c, k):
+            quant(pq[c][k], ils["p", c, k])
+
+        def ERp(g, c, t):
+            acc = mmp.tile([P, NT], F32, name="acc")
+            banks["y", g, c, t] = acc
+            for k in range(KG):
+                mx(acc[:], uq[g][k], t * P, pq[c][k], NT, k == 0, k == KG - 1)
+
+        def ERv(g, c, t):
+            nc.vector.tensor_tensor(
+                out=e_pl[g][c][:, t, :].rearrange("p (w b x) -> p w b x", w=2, x=2),
+                in0=rf[g][:, t, c * NT : (c + 1) * NT].rearrange("p (b w x) -> p w b x", w=2, x=2),
+                in1=banks["y", g, c, t][:].rearrange("p (b w x) -> p w b x", w=2, x=2),
+                op=SUB,
+            )
+
+        def ETp(g, c, h):
+            turn_pe(("e", g, c), e_pl[g][c], 0, h, True)
+
+        def ETs(g, c, h):
+            turn_out(("e", g, c), h)
+
+        def ETq(g, c):
+            quant(etq[g][c], ils["e", g, c])
+
+        def ESp(g, c, h):
+            if E_ENGINE[g][c][h] == "P":
+                through_pe(("b", g, c), e_pl[g][c], h)
+
+        def ESs(g, c, h):
+            if E_ENGINE[g][c][h] == "P":
+                through_out(("b", g, c), h)
+            else:
+                spread_half(("b", g, c), e_pl[g][c], h, E_ENGINE[g][c][h])
+
+        def ESq(g, c):
+            quant(ebq[g][c], ils["b", g, c])
+
+        def MMv(r):
+            nc.vector.tensor_tensor(out=mbf[:, r, :], in0=mb[:, r, :].bitcast(F8), in1=msc[:], op=MULT)
+
+        def MTp(g, h):
+            turn_pe(("m", g), mbf, g * KP, h)
+
+        def MTs(g, h):
+            turn_out(("m", g), h)
+
+        def MTq(g):
+            quant(mq[g], ils["m", g])
+
+        def GN(g, t):
             if g == 0:
                 uk = il_pool.tile([P, U], F32, name="uk", tag="uk", bufs=4)
             else:
-                uk = il_pool.tile([P, U], F32, name="pl", tag="pl", bufs=6, align_bytes=64)
+                uk = il_pool.tile([P, U], F32, name="e_pl", tag="e_pl", bufs=6, align_bytes=64)
             uks[g, t] = uk
-            for n in range(4):
-                cols = slice(n * 256, (n + 1) * 256)
-                engine = nc.vector if UK_ENGINE[g] == "V" else nc.gpsimd
-                engine.tensor_tensor(out=uk[:, cols], in0=u_raw[g][:, t, cols], in1=keep_b[:, cols], op=MULT)
+            if UK_ENGINE[g] == "V":
+                nc.vector.tensor_tensor(out=uk[:], in0=u_raw[g][:, t, :], in1=keep_b[:], op=MULT)
+            else:
+                for n in range(4):
+                    cols = slice(n * 256, (n + 1) * 256)
+                    nc.gpsimd.tensor_tensor(out=uk[:, cols], in0=u_raw[g][:, t, cols], in1=keep_b[:, cols], op=MULT)
 
-        def step(g, t, n):
+        def STp(g, t, n):
+            acc = mmp.tile([P, NT], F32, name="acc")
+            banks["s", g, t, n] = acc
+            cols = slice(n * NT, (n + 1) * NT)
+            for c in range(C):
+                nc.tensor.matmul_mx(
+                    out=acc[:],
+                    lhsT=etq[g][c][0][:, t * P : (t + 1) * P].bitcast(FP8X4),
+                    lhsT_scale=etq[g][c][1][:, t * P : (t + 1) * P],
+                    rhs=lw[:, c, 2 * n * NT : 2 * (n + 1) * NT].bitcast(FP4X4),
+                    rhs_scale=lsc[:, c, cols],
+                    start=c == 0,
+                    stop=c == C - 1,
+                )
+
+        def STv(g, t, n):
             uk = uks[g, t]
-            if True:
-                acc = mmp.tile([P, NT], F32, name="acc")
-                cols = slice(n * NT, (n + 1) * NT)
-                for c in range(C):
-                    nc.tensor.matmul_mx(
-                        out=acc[:],
-                        lhsT=etq[g][c][0][:, t * P : (t + 1) * P].bitcast(FP8X4),
-                        lhsT_scale=etq[g][c][1][:, t * P : (t + 1) * P],
-                        rhs=lw[:, c, 2 * n * NT : 2 * (n + 1) * NT].bitcast(FP4X4),
-                        rhs_scale=lsc[:, c, cols],
-                        start=c == 0,
-                        stop=c == C - 1,
-                    )
-                nc.vector.tensor_tensor(out=uk[:, cols], in0=acc[:], in1=uk[:, cols], op=ADD)
+            cols = slice(n * NT, (n + 1) * NT)
+            nc.vector.tensor_tensor(out=uk[:, cols], in0=banks["s", g, t, n][:], in1=uk[:, cols], op=ADD)
             dst = u_next[g * KP : (g + 1) * KP, :].rearrange("(p t) k -> p t k", t=4)
             nc.sync.dma_start(out=dst[:, t, cols], in_=uk[:, cols])
 
-        mbf = keep_tile([P, 4, B], BF16, "mbf")
-
-        def modes_mul(r):
-            nc.vector.tensor_tensor(out=mbf[:, r, :], in0=mb[:, r, :].bitcast(F8), in1=msc[:], op=MULT)
-
-        def modes_in(g):
-            il = turn(mbf, g * KP)
-            quant(mq[g], il)
-
-        def proj(c, r):
+        def PJp(c, r):
             acc = mmp.tile([P, NT], F32, name="acc")
+            banks["z", c, r] = acc
             for g in range(G):
                 mx(acc[:], mq[g], r * P, ebq[g][c], NT, g == 0, g == G - 1)
+
+        def PJs(c, r):
             zt = il_pool.tile([P, NT], F32, name="zt", tag="zt", bufs=4)
             nc.scalar.copy(
                 out=zt[:].rearrange("p (b w x) -> p b w x", w=2, x=2),
-                in_=acc[:].rearrange("p (w b x) -> p b w x", w=2, x=2),
+                in_=banks["z", c, r][:].rearrange("p (w b x) -> p b w x", w=2, x=2),
             )
-            nc.sync.dma_start(out=z[r * P : (r + 1) * P, c * NT : (c + 1) * NT], in_=zt[:])
+            dst = z.rearrange("(p r) y -> p r y", r=4)
+            nc.sync.dma_start(out=dst[:, r, c * NT : (c + 1) * NT], in_=zt[:])
 
+        def KBp(n):
+            acc = mmp.tile([P, NT], F32, name="acc")
+            banks["k", n] = acc
+            nc.tensor.matmul(out=acc[:], lhsT=ones_b[:], rhs=krow[:, n * NT : (n + 1) * NT], start=True, stop=True)
+
+        def KBs(n):
+            nc.scalar.copy(out=keep_b[:, n * NT : (n + 1) * NT], in_=banks["k", n][:])
+
+        def MSp(n):
+            acc = mmp.tile([P, NT], F32, name="acc")
+            banks["c", n] = acc
+            nc.tensor.matmul(out=acc[:], lhsT=ones[:], rhs=mrow[:, n * NT : (n + 1) * NT], start=True, stop=True)
+
+        def MSs(n):
+            nc.scalar.copy(out=msc[:, n * NT : (n + 1) * NT], in_=banks["c", n][:])
+
+        stage = {
+            "KBp": KBp, "KBs": KBs, "MSp": MSp, "MSs": MSs,
+            "UTp": UTp, "UTs": UTs, "UTq": UTq, "PIp": PIp, "PIs": PIs, "PIq": PIq, "ERp": ERp, "ERv": ERv,
+            "ETp": ETp, "ETs": ETs, "ETq": ETq, "ESp": ESp, "ESs": ESs, "ESq": ESq, "MMv": MMv, "MTp": MTp,
+            "MTs": MTs, "MTq": MTq, "GN": GN, "STp": STp, "STv": STv, "PJp": PJp, "PJs": PJs,
+        }
         for name, *args in SCHED:
-            {
-                "UT": u_in, "PI": plant_in, "ER": err, "ET": err_turn, "ES": err_spread,
-                "MM": modes_mul, "MT": modes_in, "GN": gain, "ST": step, "PJ": proj,
-            }[name](*args)
+            stage[name](*args)

from contextlib import ExitStack

import concourse.mybir as mybir
from concourse.masks import make_identity

F32 = mybir.dt.float32
BF16 = mybir.dt.bfloat16
I32 = mybir.dt.int32
U32 = mybir.dt.uint32
U8 = mybir.dt.uint8
F8 = mybir.dt.float8_e4m3fn
FP8X4 = mybir.dt.float8_e4m3fn_x4
FP4X4 = mybir.dt.float4_e2m1fn_x4
MULT = mybir.AluOpType.mult
ADD = mybir.AluOpType.add
SUB = mybir.AluOpType.subtract

B, U, Y, R = 1024, 1024, 1536, 512
P = 128
KP = 512
NT = 512
G, KG, C = B // KP, U // KP, Y // NT
PLANT_ENGINE = (("VV","SP"),("PP","SP"),("SS","SP"))
E_ENGINE = (("SP","SS","SS"),("SS","SV","SS"))
UK_ENGINE = "VV"
LOADS = (("u",0,0),("u",0,1),("k",),("p",0,0,1),("p",1,0,1),("p",0,1,3),("p",1,1,3),("r",0,0,1),("r",0,1,3),("u",1,0),("u",1,1),("m",),("s",),("l",),("r",1,0,3))
IL_BUFS = 8
SCHED = (("UTp",0,1,0),("UTp",0,1,1),("UTs",0,1,0),("UTs",0,1,1),("UTq",0,1,0),("PIp",0,0,0),("PIp",0,0,1),("PIs",0,0,0),("KBp",1),("KBs",1),("PIs",0,0,1),("UTq",0,1,1),("KBp",0),("KBs",0),("PIq",0,0),("GN",0,2),("UTp",0,0,0),("UTp",0,0,1),("UTs",0,0,0),("UTs",0,0,1),("PIp",0,1,0),("PIp",0,1,1),("PIs",0,1,0),("UTq",0,0,0),("MSp",1),("GN",0,0),("PIs",0,1,1),("PIp",1,0,0),("PIp",1,0,1),("PIs",1,0,0),("MSs",1),("UTq",0,0,1),("GN",0,1),("PIs",1,0,1),("PIq",0,1),("GN",0,3),("MSp",0),("ERp",0,0,0),("PIq",1,0),("PIp",1,1,0),("PIp",1,1,1),("PIs",1,1,0),("MSs",0),("ERv",0,0,0),("ERp",0,0,3),("PIs",1,1,1),("ERp",0,0,1),("ERv",0,0,3),("PIp",2,1,0),("PIp",2,1,1),("PIs",2,1,0),("PIq",1,1),("ERv",0,0,1),("ERp",0,0,2),("PIs",2,1,1),("ERp",0,1,2),("ERv",0,0,2),("ERp",0,1,3),("PIq",2,1),("ERv",0,1,2),("ERp",0,1,0),("ERv",0,1,3),("ERp",0,1,1),("ERv",0,1,0),("PIp",2,0,0),("PIp",2,0,1),("PIs",2,0,0),("ERv",0,1,1),("PIs",2,0,1),("ESp",0,0,0),("ESp",0,0,1),("UTp",1,1,0),("UTp",1,1,1),("ESs",0,0,1),("UTs",1,1,0),("UTs",1,1,1),("PIq",2,0),("UTp",1,0,0),("UTp",1,0,1),("UTs",1,0,0),("UTs",1,0,1),("ERp",0,2,2),("MMv",1),("ESs",0,0,0),("UTq",1,1,1),("ERv",0,2,2),("ETp",0,1,0),("ETp",0,1,1),("ETs",0,1,0),("ETs",0,1,1),("UTq",1,0,1),("ERp",0,2,0),("MMv",2),("ESq",0,0),("ERp",0,2,1),("ERv",0,2,0),("ERp",0,2,3),("ERv",0,2,1),("ETp",0,0,0),("ETp",0,0,1),("ETs",0,0,0),("ETs",0,0,1),("ERv",0,2,3),("ERp",1,0,1),("ETq",0,1),("ERp",1,0,2),("ERv",1,0,1),("ETp",0,2,0),("ETp",0,2,1),("ETs",0,2,0),("ETs",0,2,1),("ERv",1,0,2),("ERp",1,0,3),("ERp",1,0,0),("ETq",0,0),("ERv",1,0,3),("ERp",1,2,3),("ERv",1,0,0),("ERp",1,1,1),("ERv",1,2,3),("ERp",1,1,3),("ETq",0,2),("ERv",1,1,1),("ERp",1,2,0),("ERv",1,1,3),("ERp",1,2,2),("ERv",1,2,0),("ERv",1,2,2),("ESp",0,1,0),("ESp",0,1,1),("ESs",0,1,1),("ESp",0,2,0),("ESp",0,2,1),("STp",0,1,0),("STv",0,1,0),("ESs",0,2,1),("ERp",1,1,2),("ESs",0,1,0),("ERv",1,1,2),("ESs",0,2,0),("ERp",1,2,1),("MMv",0),("STp",0,2,0),("STv",0,2,0),("MMv",3),("ESq",0,1),("ERv",1,2,1),("ESq",0,2),("ESp",1,0,0),("ESp",1,0,1),("STp",0,0,1),("STv",0,0,1),("ESs",1,0,1),("ERp",1,1,0),("ERv",1,1,0),("ESp",1,1,0),("ESp",1,1,1),("STp",0,0,0),("STv",0,0,0),("ESs",1,0,0),("ESs",1,1,1),("ETp",1,0,0),("ETp",1,0,1),("ETs",1,0,0),("ETs",1,0,1),("MTp",1,0),("MTp",1,1),("MTs",1,0),("MTs",1,1),("MTq",1),("MTp",0,0),("MTp",0,1),("MTs",0,0),("MTs",0,1),("MTq",0),("ESq",1,0),("ESs",1,1,0),("STp",0,2,1),("STv",0,2,1),("ETp",1,1,0),("ETp",1,1,1),("ETs",1,1,0),("ETs",1,1,1),("STp",0,3,0),("STv",0,3,0),("ESq",1,1),("ETq",1,0),("ETp",1,2,0),("ETp",1,2,1),("ETs",1,2,0),("ETs",1,2,1),("PJp",0,0),("PJs",0,0),("PJp",0,1),("PJs",0,1),("PJp",0,2),("PJs",0,2),("ETq",1,1),("STp",0,1,1),("STv",0,1,1),("PJp",1,0),("PJs",1,0),("ETq",1,2),("GN",1,2),("PJp",1,3),("PJs",1,3),("GN",1,1),("PJp",1,2),("PJs",1,2),("ESp",1,2,0),("ESp",1,2,1),("PJp",1,1),("PJs",1,1),("ESs",1,2,1),("STp",1,2,1),("STv",1,2,1),("STp",0,3,1),("STv",0,3,1),("GN",1,0),("ESs",1,2,0),("STp",1,1,0),("STv",1,1,0),("STp",1,0,1),("STv",1,0,1),("PJp",0,3),("PJs",0,3),("ESq",1,2),("STp",1,2,0),("STv",1,2,0),("STp",1,1,1),("STv",1,1,1),("PJp",2,0),("PJs",2,0),("GN",1,3),("PJp",2,1),("PJs",2,1),("PJp",2,3),("PJs",2,3),("STp",1,3,1),("STv",1,3,1),("STp",1,3,0),("STv",1,3,0),("PJp",2,2),("PJs",2,2),("STp",1,0,0),("STv",1,0,0))
FLOPS = 2 * (B * U * Y + B * Y * U + R * B * Y)


def tile_fleet_learning_control_s8_kernel(
    tc, u, plant, ref, keep, l_words, l_scales, modes_bytes, modes_scale, u_next, z
):
    nc = tc.nc
    with ExitStack() as ctx:
        one = ctx.enter_context(tc.tile_pool(name="one", bufs=1))
        il_pool = ctx.enter_context(tc.tile_pool(name="il", bufs=1))
        trp = ctx.enter_context(tc.psum_pool(name="trp", bufs=3))
        mmp = ctx.enter_context(tc.psum_pool(name="mmp", bufs=5))

        def keep_tile(shape, dtype, name):
            return one.tile(shape, dtype, name=name, align_bytes=64)

        ident = keep_tile([P, P], F32, "ident")
        make_identity(nc, ident[:])
        ident_b = keep_tile([P, P], BF16, "ident_b")
        nc.vector.tensor_copy(out=ident_b[:], in_=ident[:])
        lsc = keep_tile([P, C, U], U8, "lsc")
        nc.gpsimd.memset(lsc[:].rearrange("p g n -> p (g n)").bitcast(I32), 0)

        ctx.enter_context(tc.manual_schedule())
        krow = il_pool.tile([P, U], BF16, name="krow", tag="zt", bufs=4)
        nc.vector.memset(krow[:].bitcast(I32), 0)
        mrow = keep_tile([P, B], F32, "mrow")
        nc.vector.memset(mrow[:], 0.0)
        ones = keep_tile([P, P], F32, "ones")
        nc.vector.memset(ones[:], 1.0)
        ones_b = keep_tile([P, P], BF16, "ones_b")
        nc.vector.memset(ones_b[:], 1.0)
        u_raw = [keep_tile([P, 4, U], BF16, f"u_raw{g}") for g in range(G)]
        pl_raw = [keep_tile([P, 4, Y], BF16, f"pl{k}") for k in range(KG)]
        rf = [keep_tile([P, 4, Y], BF16, f"rf{g}") for g in range(G)]
        mb = keep_tile([P, 4, B], U8, "mb")
        msc = keep_tile([P, B], F32, "msc")
        lw = keep_tile([P, C, 2 * U], U8, "lw")
        keep_b = keep_tile([P, U], BF16, "keep_b")

        def load_u(g, h):
            src = u[g * KP : (g + 1) * KP, :].rearrange("(p t) k -> p t k", t=4)
            nc.sync.dma_start(out=u_raw[g][:, 2 * h : 2 * h + 2, :], in_=src[:, 2 * h : 2 * h + 2, :])

        def load_plant(k, c0, c1):
            src = plant[k * KP : (k + 1) * KP, c0 * NT : c1 * NT].rearrange("(p j) y -> p j y", j=4)
            nc.sync.dma_start(out=pl_raw[k][:, :, c0 * NT : c1 * NT], in_=src)

        def load_ref(g, c0, c1):
            src = ref[g * KP : (g + 1) * KP, c0 * NT : c1 * NT].rearrange("(p t) y -> p t y", t=4)
            nc.sync.dma_start(out=rf[g][:, :, c0 * NT : c1 * NT], in_=src)

        def load_modes():
            nc.sync.dma_start(out=mb[:], in_=modes_bytes.rearrange("(p r) k -> p r k", r=4))

        def load_rows():
            nc.sync.dma_start(out=krow[0:1, :], in_=keep.rearrange("(o k) -> o k", o=1))
            nc.sync.dma_start(out=mrow[0:1, :], in_=modes_scale)

        def load_l():
            nc.sync.dma_start(out=lw[:], in_=l_words.rearrange("g p n -> p g n"))

        def load_ls():
            for q in range(4):
                nc.sync.dma_start(
                    out=lsc[32 * q : 32 * q + 4, :, :].bitcast(I32),
                    in_=l_scales[:, 4 * q : 4 * q + 4, :].rearrange("g q n -> q g n").bitcast(I32),
                )

        for name, *args in LOADS:
            {"u": load_u, "p": load_plant, "r": load_ref, "l": load_l, "s": load_ls, "m": load_modes, "k": load_rows}[name](*args)

        def codes(name):
            return keep_tile([P, NT], U32, name + "_q"), keep_tile([P, NT], U8, name + "_s")

        def quant(dst, il, h=None):
            w = slice(0, NT) if h is None else slice(h * 256, h * 256 + 256)
            e = slice(4 * w.start, 4 * w.stop)
            nc.vector.quantize_mx(out=dst[0][:, w].bitcast(FP8X4), scales=dst[1][:, w], in_=il[:, e])

        def il_tile():
            return il_pool.tile([P, 4 * NT], BF16, name="il", tag="il", bufs=IL_BUFS, align_bytes=64)

        ils = {}
        banks = {}

        def turn_pe(key, src, k0, h, sorted_words=False):
            if key not in ils:
                ils[key] = il_tile()
            tr = trp.tile([P, NT], F32, name="tr")
            banks[key, h] = tr
            for s in range(2):
                words = src[:, 2 * h + s, k0 : k0 + KP].bitcast(F32)
                for w in range(2):
                    b0 = (2 * s + w) * P
                    cols = words[:, w * P : (w + 1) * P] if sorted_words else words[:, w : KP // 2 : 2]
                    nc.tensor.transpose(tr[:, b0 : b0 + P], cols, ident[:])

        def turn_out(key, h, engine="S"):
            il = ils[key]
            copy = nc.scalar.copy if engine == "S" else nc.vector.tensor_copy
            copy(
                out=il[:, h * 1024 : (h + 1) * 1024].bitcast(F32).rearrange("p (s b u) -> p s b u", s=2, u=2),
                in_=banks[key, h][:].rearrange("p (s u b) -> p s b u", s=2, u=2),
            )

        def spread_half(key, src, h, engine):
            if key not in ils:
                ils[key] = il_tile()
            il = ils[key]
            cols = slice(h * 256, h * 256 + 256)
            out = il[:, h * 1024 : h * 1024 + 1024].rearrange("p (c i j) -> p c j i", i=4, j=4)
            in_ = src[:, :, cols].rearrange("p j (c i) -> p c j i", i=4)
            if engine == "V":
                nc.vector.tensor_copy(out=out, in_=in_)
            else:
                nc.scalar.copy(out=out, in_=in_)

        def through_pe(key, src, h):
            if key not in ils:
                ils[key] = il_tile()
            mid = trp.tile([P, 1024], BF16, name="tr")
            banks[key, h] = mid
            in_ = src[:, :, h * 256 : h * 256 + 256].rearrange("p j c -> p c j")
            for q in range(2):
                nc.tensor.matmul(
                    out=mid[:, q * NT : (q + 1) * NT],
                    lhsT=ident_b[:],
                    rhs=in_[:, q * P : (q + 1) * P, :],
                    start=True,
                    stop=True,
                )

        def through_out(key, h):
            nc.scalar.copy(out=ils[key][:, h * 1024 : (h + 1) * 1024], in_=banks[key, h][:])

        def mx(out, lhs, m0, rhs, n, start, stop):
            nc.tensor.matmul_mx(
                out=out,
                lhsT=lhs[0][:, m0 : m0 + P].bitcast(FP8X4),
                lhsT_scale=lhs[1][:, m0 : m0 + P],
                rhs=rhs[0][:, 0:n].bitcast(FP8X4),
                rhs_scale=rhs[1][:, 0:n],
                start=start,
                stop=stop,
            )

        uq = [[codes(f"u{g}{k}") for k in range(KG)] for g in range(G)]
        pq = [[codes(f"p{c}{k}") for k in range(KG)] for c in range(C)]
        etq = [[codes(f"et{g}{c}") for c in range(C)] for g in range(G)]
        ebq = [[codes(f"eb{g}{c}") for c in range(C)] for g in range(G)]
        mq = [codes(f"m{g}") for g in range(G)]
        e_pl = [
            [il_pool.tile([P, 4, NT], BF16, name="e_pl", tag="e_pl", bufs=6, align_bytes=64) for c in range(C)]
            for g in range(G)
        ]
        mbf = keep_tile([P, 4, B], BF16, "mbf")
        uks = {}

        def UTp(g, k, h):
            turn_pe(("u", g, k), u_raw[g], k * KP, h)

        def UTs(g, k, h):
            turn_out(("u", g, k), h)

        def UTq(g, k, h):
            quant(uq[g][k], ils["u", g, k], h if g == 0 else None)

        def PIp(c, k, h):
            if PLANT_ENGINE[c][k][h] == "P":
                through_pe(("p", c, k), pl_raw[k][:, :, c * NT : (c + 1) * NT], h)

        def PIs(c, k, h):
            if PLANT_ENGINE[c][k][h] == "P":
                through_out(("p", c, k), h)
            else:
                spread_half(("p", c, k), pl_raw[k][:, :, c * NT : (c + 1) * NT], h, PLANT_ENGINE[c][k][h])

        def PIq(c, k):
            quant(pq[c][k], ils["p", c, k])

        def ERp(g, c, t):
            acc = mmp.tile([P, NT], F32, name="acc")
            banks["y", g, c, t] = acc
            for k in range(KG):
                mx(acc[:], uq[g][k], t * P, pq[c][k], NT, k == 0, k == KG - 1)

        def ERv(g, c, t):
            nc.vector.tensor_tensor(
                out=e_pl[g][c][:, t, :].rearrange("p (w b x) -> p w b x", w=2, x=2),
                in0=rf[g][:, t, c * NT : (c + 1) * NT].rearrange("p (b w x) -> p w b x", w=2, x=2),
                in1=banks["y", g, c, t][:].rearrange("p (b w x) -> p w b x", w=2, x=2),
                op=SUB,
            )

        def ETp(g, c, h):
            turn_pe(("e", g, c), e_pl[g][c], 0, h, True)

        def ETs(g, c, h):
            turn_out(("e", g, c), h)

        def ETq(g, c):
            quant(etq[g][c], ils["e", g, c])

        def ESp(g, c, h):
            if E_ENGINE[g][c][h] == "P":
                through_pe(("b", g, c), e_pl[g][c], h)

        def ESs(g, c, h):
            if E_ENGINE[g][c][h] == "P":
                through_out(("b", g, c), h)
            else:
                spread_half(("b", g, c), e_pl[g][c], h, E_ENGINE[g][c][h])

        def ESq(g, c):
            quant(ebq[g][c], ils["b", g, c])

        def MMv(r):
            nc.vector.tensor_tensor(out=mbf[:, r, :], in0=mb[:, r, :].bitcast(F8), in1=msc[:], op=MULT)

        def MTp(g, h):
            turn_pe(("m", g), mbf, g * KP, h)

        def MTs(g, h):
            turn_out(("m", g), h)

        def MTq(g):
            quant(mq[g], ils["m", g])

        def GN(g, t):
            if g == 0:
                uk = il_pool.tile([P, U], F32, name="uk", tag="uk", bufs=4)
            else:
                uk = il_pool.tile([P, U], F32, name="e_pl", tag="e_pl", bufs=6, align_bytes=64)
            uks[g, t] = uk
            if UK_ENGINE[g] == "V":
                nc.vector.tensor_tensor(out=uk[:], in0=u_raw[g][:, t, :], in1=keep_b[:], op=MULT)
            else:
                for n in range(4):
                    cols = slice(n * 256, (n + 1) * 256)
                    nc.gpsimd.tensor_tensor(out=uk[:, cols], in0=u_raw[g][:, t, cols], in1=keep_b[:, cols], op=MULT)

        def STp(g, t, n):
            acc = mmp.tile([P, NT], F32, name="acc")
            banks["s", g, t, n] = acc
            cols = slice(n * NT, (n + 1) * NT)
            for c in range(C):
                nc.tensor.matmul_mx(
                    out=acc[:],
                    lhsT=etq[g][c][0][:, t * P : (t + 1) * P].bitcast(FP8X4),
                    lhsT_scale=etq[g][c][1][:, t * P : (t + 1) * P],
                    rhs=lw[:, c, 2 * n * NT : 2 * (n + 1) * NT].bitcast(FP4X4),
                    rhs_scale=lsc[:, c, cols],
                    start=c == 0,
                    stop=c == C - 1,
                )

        def STv(g, t, n):
            uk = uks[g, t]
            cols = slice(n * NT, (n + 1) * NT)
            nc.vector.tensor_tensor(out=uk[:, cols], in0=banks["s", g, t, n][:], in1=uk[:, cols], op=ADD)
            dst = u_next[g * KP : (g + 1) * KP, :].rearrange("(p t) k -> p t k", t=4)
            nc.sync.dma_start(out=dst[:, t, cols], in_=uk[:, cols])

        def PJp(c, r):
            acc = mmp.tile([P, NT], F32, name="acc")
            banks["z", c, r] = acc
            for g in range(G):
                mx(acc[:], mq[g], r * P, ebq[g][c], NT, g == 0, g == G - 1)

        def PJs(c, r):
            zt = il_pool.tile([P, NT], F32, name="zt", tag="zt", bufs=4)
            nc.scalar.copy(
                out=zt[:].rearrange("p (b w x) -> p b w x", w=2, x=2),
                in_=banks["z", c, r][:].rearrange("p (w b x) -> p b w x", w=2, x=2),
            )
            dst = z.rearrange("(p r) y -> p r y", r=4)
            nc.sync.dma_start(out=dst[:, r, c * NT : (c + 1) * NT], in_=zt[:])

        def KBp(n):
            acc = mmp.tile([P, NT], F32, name="acc")
            banks["k", n] = acc
            nc.tensor.matmul(out=acc[:], lhsT=ones_b[:], rhs=krow[:, n * NT : (n + 1) * NT], start=True, stop=True)

        def KBs(n):
            nc.scalar.copy(out=keep_b[:, n * NT : (n + 1) * NT], in_=banks["k", n][:])

        def MSp(n):
            acc = mmp.tile([P, NT], F32, name="acc")
            banks["c", n] = acc
            nc.tensor.matmul(out=acc[:], lhsT=ones[:], rhs=mrow[:, n * NT : (n + 1) * NT], start=True, stop=True)

        def MSs(n):
            nc.scalar.copy(out=msc[:, n * NT : (n + 1) * NT], in_=banks["c", n][:])

        stage = {
            "KBp": KBp, "KBs": KBs, "MSp": MSp, "MSs": MSs,
            "UTp": UTp, "UTs": UTs, "UTq": UTq, "PIp": PIp, "PIs": PIs, "PIq": PIq, "ERp": ERp, "ERv": ERv,
            "ETp": ETp, "ETs": ETs, "ETq": ETq, "ESp": ESp, "ESs": ESs, "ESq": ESq, "MMv": MMv, "MTp": MTp,
            "MTs": MTs, "MTq": MTq, "GN": GN, "STp": STp, "STv": STv, "PJp": PJp, "PJs": PJs,
        }
        for name, *args in SCHED:
            stage[name](*args)
